import numpy as np
import ml_dtypes


def mxq(x, axis, fmt="e4m3"):
    dtype, down = {"e4m3": (ml_dtypes.float8_e4m3fn, 7), "e5m2": (ml_dtypes.float8_e5m2, 14)}[fmt]
    v = np.moveaxis(np.asarray(x, np.float32).astype(ml_dtypes.bfloat16).astype(np.float64), axis, -1)
    blocks = v.reshape(v.shape[:-1] + (-1, 32))
    amax = np.abs(blocks).max(-1, keepdims=True)
    byte = np.maximum(np.where(amax > 0, np.frexp(amax)[1] - 1 + 127, 0) - down, 1)
    scale = np.exp2(byte - 127.0)
    codes = (blocks / scale).astype(np.float32).astype(dtype).astype(np.float64)
    return np.moveaxis((codes * scale).reshape(v.shape), -1, axis)


WIDE = False


def mx_kscale(k):
    if not WIDE:
        return np.ones(k)
    levels = np.array([10, -10, 5, -5, 0])
    if k % 512:
        return np.exp2(np.random.permutation(np.resize(levels, k // 32))).repeat(32)
    a = np.empty((k // 512, 16))
    for p in range(k // 512):
        a[p, :8] = np.random.permutation(np.resize(levels, 8))
        for g in range(8):
            far = levels[np.abs(levels - a[p, g]) >= 10]
            a[p, g + 8] = far[np.random.randint(len(far))]
    return np.exp2(a.ravel()).repeat(32)


def f64(x):
    return np.asarray(x).astype(np.float64)


def striped8(idx):
    return np.concatenate([x.reshape(-1, 16).T for x in idx]).astype(np.uint16)


def runs(offs, k):
    lists = np.stack([offs[16 * r : 16 * r + 16].T.reshape(-1) for r in range(8)]).astype(np.int64)
    return lists[np.arange(k) % 512 // 64]


def pack_weight(w):
    k, n = w.shape
    w = f64(np.asarray(w, np.float32).astype(ml_dtypes.bfloat16)).reshape(k // 32, 32, n)
    amax = np.abs(w).max(1)
    byte = np.clip(np.where(amax > 0, np.frexp(amax)[1] - 1 + 127 - 7, 1), 1, 254)
    scaled = (w * np.exp2(127.0 - byte)[:, None, :]).reshape(k, n).astype(np.float32)
    words = np.ascontiguousarray(scaled.reshape(k // 512, 128, 4, n).transpose(0, 1, 3, 2)).astype(ml_dtypes.float8_e4m3fn).view(np.uint8)
    return words, np.ascontiguousarray(byte.astype(np.uint8).reshape(k // 512, 16, n))


def unpack_weight(words, scales):
    g, p, n, _ = words.shape
    vals = np.ascontiguousarray(words).view(ml_dtypes.float8_e4m3fn).astype(np.float64) * np.repeat(np.exp2(scales.astype(np.float64) - 127.0), 8, axis=1)[..., None]
    return vals.transpose(0, 1, 3, 2).reshape(g * 512, n)


def sigmoid(v):
    return 1.0 / (1.0 + np.exp(-np.maximum(v, -700.0)))


K, T, S, N, H, W = 512, 2048, 512, 512, 512, 256


def setup_inputs():
    n = np.random.standard_normal
    s = mx_kscale(K)[:, None]
    u = mx_kscale(H)
    packed_xT = pack_weight(n((K, T)) * s)
    perm = np.stack([np.random.permutation(S) for _ in range(8)])
    return {
        "x_words": packed_xT[0],
        "x_scales": packed_xT[1],
        "w1": (n((K, H)) / np.sqrt(K) / s).astype(np.float32),
        "gn": (np.random.uniform(0.5, 1.5, (H, 1)) * u[:, None]).astype(np.float32),
        "w2": (n((H, N)) / np.sqrt(H) / u[:, None]).astype(np.float32),
        "offs": striped8(np.random.randint(0, T, (8, S))),
        "n1": striped8(np.stack([np.random.permutation(S) for _ in range(8)])),
        "n2": striped8(np.stack([np.random.permutation(S) for _ in range(8)])),
        "n3": striped8(perm[:, :W]),
        "n4": striped8(perm[:, W:]),
    }


def reference(x_words, x_scales, w1, gn, w2, offs, n1, n2, n3, n4):
    xq = unpack_weight(x_words, x_scales)[np.arange(K)[:, None], runs(offs, K)]
    y = mxq(f64(w1), 0, "e4m3").T @ xq
    sm = np.maximum(y, y[np.arange(H)[:, None], runs(n2, H)])
    ds = np.zeros((H, S))
    ds[np.arange(H)[:, None], runs(n1, H)] = sm
    z = f64(gn) * (ds * sigmoid(y))
    h = mxq(f64(w2), 0, "e4m3").T @ mxq(z, 0, "e4m3")
    pb = h[np.arange(N)[:, None], runs(n4, N)]
    pa = h[np.arange(N)[:, None], runs(n3, N)]
    rb = pb * sigmoid(pb - pa)
    ra = pa * sigmoid(pa - pb)
    ds2 = np.zeros((N, S))
    ds2[np.arange(N)[:, None], runs(n3, N)] = ra
    out = ds2.copy()
    out[np.arange(N)[:, None], runs(n4, N)] = rb
    return out

@@ -1,0 +1,298 @@
+from contextlib import ExitStack
+
+import concourse.mybir as mybir
+from concourse.masks import make_identity
+
+F32 = mybir.dt.float32
+BF16 = mybir.dt.bfloat16
+I32 = mybir.dt.int32
+U32 = mybir.dt.uint32
+U16 = mybir.dt.uint16
+U8 = mybir.dt.uint8
+FP8X4 = mybir.dt.float8_e4m3fn_x4
+ACT = mybir.ActivationFunctionType
+ALU = mybir.AluOpType
+
+P = 128
+PACK = 4
+T = 2048
+S = 512
+HALF = S // 2
+FLOPS = 2 * 2 * 512 * 512 * 512
+
+
+def tile_picked_hashsendgduel_none_p_kernel(
+    tc, x_words, x_scales, w1, gn, w2, offs, n1, n2, n3, n4, out
+):
+    nc = tc.nc
+    with ExitStack() as ctx:
+        lists = ctx.enter_context(tc.tile_pool(name="lists", bufs=1))
+        sb = ctx.enter_context(tc.tile_pool(name="sb", bufs=1))
+        psum = ctx.enter_context(tc.psum_pool(name="psum", bufs=1))
+
+        def bank(b, width, name):
+            return psum.tile([P, width], F32, tag="bank%d" % b, name=name)
+
+        def f32(width, name):
+            return sb.tile([P, width], F32, name=name, align_bytes=64)
+
+        offs_t = lists.tile([P, S // 16], U16, name="offs_t")
+        n1_t = lists.tile([P, S // 16], U16, name="n1_t")
+        n2_t = lists.tile([P, S // 16], U16, name="n2_t")
+        n3_t = lists.tile([P, HALF // 16], U16, name="n3_t")
+        n4_t = lists.tile([P, HALF // 16], U16, name="n4_t")
+
+        scale_table = sb.tile([P, T], U8, tag="early", name="scale_table", align_bytes=64)
+        x_plane = sb.tile([P, S], U8, name="x_plane", align_bytes=64)
+        nc.vector.memset(scale_table[:].bitcast(I32), 0)
+        nc.vector.memset(x_plane[:].bitcast(I32), 0)
+        nc.scalar.dma_start(out=scale_table[:].bitcast(I32)[0:P:8, :], in_=x_scales[0].bitcast(I32))
+
+        w1_raw = sb.tile([P, PACK, S], F32, tag="w_raw", name="w1_raw", align_bytes=64)
+        word_table = sb.tile([P, T], I32, name="word_table", align_bytes=64)
+        nc.sync.dma_start(offs_t[:], offs)
+        nc.sync.dma_start(out=w1_raw[:], in_=w1.rearrange("(p j) c -> p j c", j=PACK))
+        nc.sync.dma_start(n2_t[:], n2)
+        nc.sync.dma_start(n1_t[:], n1)
+        nc.sync.dma_start(out=word_table[:], in_=x_words[0].rearrange("p c r -> p (c r)").bitcast(I32))
+        nc.sync.dma_start(n3_t[:], n3)
+        nc.sync.dma_start(n4_t[:], n4)
+        ident = f32(P, "ident")
+        make_identity(nc, ident[:])
+
+        picked_scales = sb.tile([P, S], U8, name="picked_scales", align_bytes=64)
+        nc.vector.tensor_copy(picked_scales[:], scale_table[:].indirect(offs_t[:]))
+        for q in range(4):
+            nc.scalar.dma_start(
+                out=x_plane[:].bitcast(I32)[32 * q : 32 * q + 4, :],
+                in_=picked_scales[:].bitcast(I32)[32 * q : 32 * q + 32 : 8, :],
+            )
+        gain = sb.tile([P, PACK], F32, tag="early", name="gain", align_bytes=64)
+        nc.sync.dma_start(out=gain[:], in_=gn.rearrange("(p t) o -> p (t o)", t=PACK))
+
+        def deal(copy, grouped, raw, th):
+            copy(
+                grouped[:].rearrange("p (th tl m j) -> p th m j tl", th=2, tl=2, j=PACK)[:, th],
+                raw[:].rearrange("p j (m th tl) -> p th m j tl", th=2, tl=2)[:, th],
+            )
+
+        w1_bf = sb.tile([P, PACK * S], BF16, name="w1_bf", align_bytes=64)
+        w1_codes = sb.tile([P, S], U32, name="w1_codes", align_bytes=64)
+        w1_plane = sb.tile([P, S], U8, name="w1_plane", align_bytes=64)
+        for th in range(2):
+            deal(nc.vector.tensor_copy, w1_bf, w1_raw, th)
+        nc.vector.quantize_mx(out=w1_codes[:].bitcast(FP8X4), scales=w1_plane[:], in_=w1_bf[:])
+
+        w2_raw = sb.tile([P, PACK, S], F32, tag="w_raw", name="w2_raw", align_bytes=64)
+        nc.sync.dma_start(out=w2_raw[:], in_=w2.rearrange("(p j) c -> p j c", j=PACK))
+
+        x_codes = sb.tile([P, S], U32, name="x_codes", align_bytes=64)
+        halves = [slice(0, HALF), slice(HALF, S)]
+        for a in range(2):
+            nc.vector.tensor_copy(
+                x_codes[:, halves[a]], word_table[:].bitcast(U32).indirect(offs_t[:, 16 * a : 16 * a + 16])
+            )
+
+        def product(acc, codes, plane, t, rhs, rhs_plane):
+            nc.tensor.matmul_mx(
+                out=acc,
+                lhsT=codes[:, P * t : P * (t + 1)].bitcast(FP8X4),
+                lhsT_scale=plane[:, P * t : P * (t + 1)],
+                rhs=rhs.bitcast(FP8X4),
+                rhs_scale=rhs_plane,
+                start=True,
+                stop=True,
+            )
+
+        order = [1, 2, 3, 0]
+        y_ps = {}
+        for a in range(2):
+            for u in range(2):
+                y_ps[u, a] = bank(2 * u + a, HALF, "y_ps%d%d" % (u, a))
+                product(y_ps[u, a][:], w1_codes, w1_plane, order[u], x_codes[:, halves[a]], x_plane[:, halves[a]])
+        for u in (2, 3):
+            y_ps[u] = bank(2 + u, S, "y_ps%d" % u)
+            product(y_ps[u][:], w1_codes, w1_plane, order[u], x_codes[:], x_plane[:])
+
+        y_win = [f32(S, "y_win0"), f32(S, "y_win1"), f32(2 * S, "y_win2"), f32(2 * S, "y_win3")]
+        twin0, twin3 = f32(S, "y_twin0"), f32(S, "y_twin3")
+        y_twin = [twin0[:], y_win[2][:, S:], y_win[3][:, S:], twin3[:]]
+        left, right = f32(PACK * S, "left"), f32(PACK * S, "right")
+
+        def left_slot(t):
+            return left[:, S * t : S * (t + 1)]
+
+        def right_slot(t):
+            return right[:, S * (3 - t) : S * (4 - t)]
+
+        ds_win = [f32(2 * S, "ds_win0"), f32(2 * S, "ds_win1"), right, left]
+        gap = [f32(S, "gap%d" % u) for u in range(4)]
+        lift = [f32(S, "lift%d" % u) for u in range(4)]
+        sig_raw = {u: f32(S, "sig_raw%d" % u) for u in (2, 3)}
+
+        def gather_gap(u):
+            if u < 2:
+                for a in range(2):
+                    nc.vector.tensor_tensor(
+                        gap[u][:, halves[a]], y_win[u][:].indirect(n2_t[:, 16 * a : 16 * a + 16]),
+                        y_twin[u][:, halves[a]], ALU.subtract,
+                    )
+            else:
+                nc.vector.tensor_tensor(gap[u][:], y_win[u][:].indirect(n2_t[:]), y_twin[u], ALU.subtract)
+
+        def relu(u):
+            nc.scalar.activation(lift[u][:], gap[u][:], ACT.Relu)
+
+        def send(u):
+            nc.vector.tensor_tensor(ds_win[u][:].indirect(n1_t[:]), y_win[u][:, :S], lift[u][:], ALU.add)
+
+        def evacuate(u):
+            nc.scalar.copy(y_win[u][:, :S], y_ps[u][:])
+            nc.scalar.copy(y_twin[u], y_ps[u][:])
+
+        def scaled(dst, src, t):
+            nc.scalar.activation(dst, src, ACT.Copy, scale=gain[:, t : t + 1])
+
+        lo, hi = halves
+        nc.scalar.activation(right_slot(order[0])[:, lo], y_ps[0, 0][:], ACT.Sigmoid)
+        nc.scalar.copy(y_win[0][:, lo], y_ps[0, 0][:])
+        nc.vector.tensor_copy(y_win[1][:, lo], y_ps[1, 0][:])
+        nc.vector.tensor_copy(y_twin[1][:, lo], y_ps[1, 0][:])
+        nc.vector.tensor_copy(y_twin[0][:, lo], y_win[0][:, lo])
+        nc.scalar.copy(y_win[0][:, hi], y_ps[0, 1][:])
+        nc.scalar.copy(y_twin[0][:, hi], y_ps[0, 1][:])
+        nc.scalar.copy(y_win[1][:, hi], y_ps[1, 1][:])
+        nc.scalar.copy(y_twin[1][:, hi], y_ps[1, 1][:])
+        gather_gap(0)
+        gather_gap(1)
+        relu(0)
+        send(0)
+        evacuate(2)
+        gather_gap(2)
+        relu(1)
+        send(1)
+        evacuate(3)
+        gather_gap(3)
+        nc.scalar.activation(right_slot(order[0])[:, hi], y_twin[0][:, hi], ACT.Sigmoid)
+        nc.scalar.activation(right_slot(order[1]), y_twin[1], ACT.Sigmoid)
+        nc.scalar.activation(sig_raw[3][:], y_twin[3], ACT.Sigmoid)
+        relu(2)
+        scaled(right_slot(order[3]), sig_raw[3][:], order[3])
+        send(2)
+        scaled(left_slot(order[0]), ds_win[0][:, :S], order[0])
+        nc.scalar.activation(sig_raw[2][:], y_twin[2], ACT.Sigmoid)
+        scaled(left_slot(order[2]), sig_raw[2][:], order[2])
+        scaled(left_slot(order[1]), ds_win[1][:, :S], order[1])
+        relu(3)
+        send(3)
+
+        w2_bf = sb.tile([P, PACK * S], BF16, name="w2_bf", align_bytes=64)
+        w2_codes = sb.tile([P, S], U32, name="w2_codes", align_bytes=64)
+        w2_plane = sb.tile([P, S], U8, name="w2_plane", align_bytes=64)
+        for th in range(2):
+            deal(nc.scalar.copy, w2_bf, w2_raw, th)
+
+        def quantize_w2(t):
+            nc.vector.quantize_mx(
+                out=w2_codes[:, P * t : P * (t + 1)].bitcast(FP8X4),
+                scales=w2_plane[:, P * t : P * (t + 1)],
+                in_=w2_bf[:, S * t : S * (t + 1)],
+            )
+
+        z_bf = [sb.tile([P, PACK * HALF], BF16, name="z_bf%d" % a, align_bytes=64) for a in range(2)]
+        z_codes = sb.tile([P, S], U32, name="z_codes", align_bytes=64)
+        z_plane = sb.tile([P, S], U8, name="z_plane", align_bytes=64)
+        for a in range(2):
+            pairs = slice(a * HALF // 2, (a + 1) * HALF // 2)
+            nc.vector.tensor_tensor(
+                z_bf[a][:].rearrange("p (c i t) -> p c t i", i=2, t=PACK),
+                left[:].rearrange("p (t c i) -> p c t i", t=PACK, i=2)[:, pairs],
+                right[:].rearrange("p (t c i) -> p c t i", t=PACK, i=2)[:, pairs, ::-1, :],
+                ALU.mult,
+            )
+
+        def quantize_z(a):
+            nc.vector.quantize_mx(
+                out=z_codes[:, halves[a]].bitcast(FP8X4), scales=z_plane[:, halves[a]], in_=z_bf[a][:]
+            )
+
+        quantize_z(0)
+        quantize_w2(0)
+        quantize_z(1)
+        for t in (1, 2, 3):
+            quantize_w2(t)
+
+        h_win = [f32(S, "h_win%d" % t) for t in range(4)]
+        for a in range(2):
+            h_half = bank(6 + a, HALF, "h_ps0%d" % a)
+            product(h_half[:], w2_codes, w2_plane, 0, z_codes[:, halves[a]], z_plane[:, halves[a]])
+            nc.scalar.copy(h_win[0][:, halves[a]], h_half[:])
+        h_ps = {}
+        for t in (1, 2, 3):
+            h_ps[t] = bank(t - 1, S, "h_ps%d" % t)
+            product(h_ps[t][:], w2_codes, w2_plane, t, z_codes[:], z_plane[:])
+
+        pa = [f32(HALF, "pa%d" % t) for t in range(4)]
+        pb = [f32(HALF, "pb%d" % t) for t in range(4)]
+        minus_pb = [f32(HALF, "minus_pb%d" % t) for t in range(4)]
+        turned = [f32(HALF, "turned%d" % t) for t in range(4)]
+        sa = [f32(HALF, "sa%d" % t) for t in range(4)]
+        sig_b = [f32(HALF, "sb%d" % t) for t in range(4)]
+        o_win = [f32(S, "o_win%d" % t) for t in range(4)]
+        diff = {}
+        turned_ps = {}
+        blocks = [slice(0, P), slice(P, 2 * P)]
+        out_rows = out.rearrange("(p t) c -> p t c", t=PACK)
+
+        def fetch(t):
+            nc.vector.tensor_copy(pb[t][:], h_win[t][:].indirect(n4_t[:]))
+            nc.vector.tensor_copy(pa[t][:], h_win[t][:].indirect(n3_t[:]))
+
+        def h_out(t):
+            nc.scalar.copy(h_win[t][:], h_ps[t][:])
+
+        def negate(t):
+            nc.scalar.activation(minus_pb[t][:], pb[t][:], ACT.Copy, scale=-1.0)
+            turned_ps[t] = bank(3 + t % 2, HALF, "turned_ps%d" % t)
+            for blk in blocks:
+                nc.tensor.matmul(turned_ps[t][:, blk], pa[t][:, blk], ident[:], start=True, stop=False, is_transpose=True)
+                nc.tensor.matmul(turned_ps[t][:, blk], minus_pb[t][:, blk], ident[:], start=False, stop=True, is_transpose=True)
+
+        def turn_back(t):
+            nc.scalar.copy(turned[t][:], turned_ps[t][:])
+            diff[t] = bank(5 + t % 2, HALF, "diff%d" % t)
+            for blk in blocks:
+                nc.tensor.transpose(diff[t][:, blk], turned[t][:, blk], ident[:])
+
+        def put_a(t):
+            nc.scalar.activation(sa[t][:], diff[t][:], ACT.Sigmoid)
+            nc.vector.tensor_tensor(o_win[t][:].indirect(n3_t[:]), pa[t][:], sa[t][:], ALU.mult)
+
+        def put_b(t):
+            nc.scalar.activation(sig_b[t][:], diff[t][:], ACT.Sigmoid, scale=-1.0)
+            nc.vector.tensor_tensor(o_win[t][:].indirect(n4_t[:]), pb[t][:], sig_b[t][:], ALU.mult)
+            nc.sync.dma_start(out=out_rows[:, t, :], in_=o_win[t][:])
+
+        fetch(0)
+        h_out(1)
+        fetch(1)
+        h_out(2)
+        fetch(2)
+        negate(0)
+        h_out(3)
+        fetch(3)
+        turn_back(0)
+        negate(1)
+        put_a(0)
+        turn_back(1)
+        negate(2)
+        put_a(1)
+        put_b(0)
+        turn_back(2)
+        negate(3)
+        put_a(2)
+        put_b(1)
+        turn_back(3)
+        put_a(3)
+        put_b(2)
+        put_b(3)

@@ -44,24 +44,41 @@ def tile_picked_hashsendgduel_none_p_kernel(
 
         scale_table = sb.tile([P, T], U8, tag="early", name="scale_table", align_bytes=64)
         x_plane = sb.tile([P, S], U8, name="x_plane", align_bytes=64)
-        nc.vector.memset(scale_table[:].bitcast(I32), 0)
+        nc.gpsimd.memset(scale_table[:].bitcast(I32), 0)
         nc.vector.memset(x_plane[:].bitcast(I32), 0)
         nc.scalar.dma_start(out=scale_table[:].bitcast(I32)[0:P:8, :], in_=x_scales[0].bitcast(I32))
 
-        w1_raw = sb.tile([P, PACK, S], F32, tag="w_raw", name="w1_raw", align_bytes=64)
+        w1_lo = sb.tile([P, PACK, HALF], F32, name="w1_lo", align_bytes=64)
+        w1_hi = sb.tile([P, PACK, HALF], F32, tag="w_raw", name="w1_hi", align_bytes=64)
+        w1_rows = w1.rearrange("(p j) c -> p j c", j=PACK)
         word_table = sb.tile([P, T], I32, name="word_table", align_bytes=64)
         nc.sync.dma_start(offs_t[:], offs)
-        nc.sync.dma_start(out=w1_raw[:], in_=w1.rearrange("(p j) c -> p j c", j=PACK))
+        nc.sync.dma_start(out=w1_lo[:], in_=w1_rows[:, :, :HALF])
         nc.sync.dma_start(n2_t[:], n2)
         nc.sync.dma_start(n1_t[:], n1)
-        nc.sync.dma_start(out=word_table[:], in_=x_words[0].rearrange("p c r -> p (c r)").bitcast(I32))
         nc.sync.dma_start(n3_t[:], n3)
         nc.sync.dma_start(n4_t[:], n4)
+        nc.sync.dma_start(out=w1_hi[:], in_=w1_rows[:, :, HALF:])
+        nc.sync.dma_start(out=word_table[:], in_=x_words[0].rearrange("p c r -> p (c r)").bitcast(I32))
         ident = f32(P, "ident")
         make_identity(nc, ident[:])
 
         picked_scales = sb.tile([P, S], U8, name="picked_scales", align_bytes=64)
         nc.vector.tensor_copy(picked_scales[:], scale_table[:].indirect(offs_t[:]))
+
+        def deal(copy, grouped, raw, th, ms):
+            copy(
+                grouped[:].rearrange("p (th tl m j) -> p th m j tl", th=2, tl=2, j=PACK)[:, th, ms],
+                raw[:].rearrange("p j (m th tl) -> p th m j tl", th=2, tl=2)[:, th],
+            )
+
+        w1_bf = sb.tile([P, PACK * S], BF16, name="w1_bf", align_bytes=64)
+        w1_codes = sb.tile([P, S], U32, name="w1_codes", align_bytes=64)
+        w1_plane = sb.tile([P, S], U8, name="w1_plane", align_bytes=64)
+        deal(nc.vector.tensor_copy, w1_bf, w1_lo, 0, slice(0, 64))
+        deal(nc.vector.tensor_copy, w1_bf, w1_lo, 1, slice(0, 64))
+        deal(nc.vector.tensor_copy, w1_bf, w1_hi, 0, slice(64, 128))
+        deal(nc.vector.tensor_copy, w1_bf, w1_hi, 1, slice(64, 128))
         for q in range(4):
             nc.scalar.dma_start(
                 out=x_plane[:].bitcast(I32)[32 * q : 32 * q + 4, :],
@@ -69,19 +86,11 @@ def tile_picked_hashsendgduel_none_p_kernel(
             )
         gain = sb.tile([P, PACK], F32, tag="early", name="gain", align_bytes=64)
         nc.sync.dma_start(out=gain[:], in_=gn.rearrange("(p t) o -> p (t o)", t=PACK))
-
-        def deal(copy, grouped, raw, th):
-            copy(
-                grouped[:].rearrange("p (th tl m j) -> p th m j tl", th=2, tl=2, j=PACK)[:, th],
-                raw[:].rearrange("p j (m th tl) -> p th m j tl", th=2, tl=2)[:, th],
-            )
-
-        w1_bf = sb.tile([P, PACK * S], BF16, name="w1_bf", align_bytes=64)
-        w1_codes = sb.tile([P, S], U32, name="w1_codes", align_bytes=64)
-        w1_plane = sb.tile([P, S], U8, name="w1_plane", align_bytes=64)
         for th in range(2):
-            deal(nc.vector.tensor_copy, w1_bf, w1_raw, th)
-        nc.vector.quantize_mx(out=w1_codes[:].bitcast(FP8X4), scales=w1_plane[:], in_=w1_bf[:])
+            cols = slice(HALF * th, HALF * (th + 1))
+            nc.vector.quantize_mx(
+                out=w1_codes[:, cols].bitcast(FP8X4), scales=w1_plane[:, cols], in_=w1_bf[:, 2 * S * th : 2 * S * (th + 1)]
+            )
 
         w2_raw = sb.tile([P, PACK, S], F32, tag="w_raw", name="w2_raw", align_bytes=64)
         nc.sync.dma_start(out=w2_raw[:], in_=w2.rearrange("(p j) c -> p j c", j=PACK))
@@ -154,14 +163,14 @@ def tile_picked_hashsendgduel_none_p_kernel(
             nc.scalar.activation(dst, src, ACT.Copy, scale=gain[:, t : t + 1])
 
         lo, hi = halves
-        nc.scalar.activation(right_slot(order[0])[:, lo], y_ps[0, 0][:], ACT.Sigmoid)
-        nc.scalar.copy(y_win[0][:, lo], y_ps[0, 0][:])
+        nc.scalar.activation(right_slot(order[1])[:, lo], y_ps[1, 0][:], ACT.Sigmoid)
+        nc.vector.tensor_copy(y_win[0][:, lo], y_ps[0, 0][:])
+        nc.vector.tensor_copy(y_twin[0][:, lo], y_ps[0, 0][:])
         nc.vector.tensor_copy(y_win[1][:, lo], y_ps[1, 0][:])
-        nc.vector.tensor_copy(y_twin[1][:, lo], y_ps[1, 0][:])
-        nc.vector.tensor_copy(y_twin[0][:, lo], y_win[0][:, lo])
         nc.scalar.copy(y_win[0][:, hi], y_ps[0, 1][:])
         nc.scalar.copy(y_twin[0][:, hi], y_ps[0, 1][:])
         nc.scalar.copy(y_win[1][:, hi], y_ps[1, 1][:])
+        nc.scalar.copy(y_twin[1][:, lo], y_ps[1, 0][:])
         nc.scalar.copy(y_twin[1][:, hi], y_ps[1, 1][:])
         gather_gap(0)
         gather_gap(1)
@@ -173,8 +182,8 @@ def tile_picked_hashsendgduel_none_p_kernel(
         send(1)
         evacuate(3)
         gather_gap(3)
-        nc.scalar.activation(right_slot(order[0])[:, hi], y_twin[0][:, hi], ACT.Sigmoid)
-        nc.scalar.activation(right_slot(order[1]), y_twin[1], ACT.Sigmoid)
+        nc.scalar.activation(right_slot(order[0]), y_twin[0], ACT.Sigmoid)
+        nc.scalar.activation(right_slot(order[1])[:, hi], y_twin[1][:, hi], ACT.Sigmoid)
         nc.scalar.activation(sig_raw[3][:], y_twin[3], ACT.Sigmoid)
         relu(2)
         scaled(right_slot(order[3]), sig_raw[3][:], order[3])
@@ -190,7 +199,7 @@ def tile_picked_hashsendgduel_none_p_kernel(
         w2_codes = sb.tile([P, S], U32, name="w2_codes", align_bytes=64)
         w2_plane = sb.tile([P, S], U8, name="w2_plane", align_bytes=64)
         for th in range(2):
-            deal(nc.scalar.copy, w2_bf, w2_raw, th)
+            deal(nc.scalar.copy, w2_bf, w2_raw, th, slice(0, P))
 
         def quantize_w2(t):
             nc.vector.quantize_mx(
@@ -234,7 +243,7 @@ def tile_picked_hashsendgduel_none_p_kernel(
 
         pa = [f32(HALF, "pa%d" % t) for t in range(4)]
         pb = [f32(HALF, "pb%d" % t) for t in range(4)]
-        minus_pb = [f32(HALF, "minus_pb%d" % t) for t in range(4)]
+        minus_pb = {}
         turned = [f32(HALF, "turned%d" % t) for t in range(4)]
         sa = [f32(HALF, "sa%d" % t) for t in range(4)]
         sig_b = [f32(HALF, "sb%d" % t) for t in range(4)]
@@ -252,8 +261,9 @@ def tile_picked_hashsendgduel_none_p_kernel(
             nc.scalar.copy(h_win[t][:], h_ps[t][:])
 
         def negate(t):
+            minus_pb[t] = sb.tile([P, HALF], F32, tag="minus_pb", name="minus_pb%d" % t, align_bytes=64)
             nc.scalar.activation(minus_pb[t][:], pb[t][:], ACT.Copy, scale=-1.0)
-            turned_ps[t] = bank(3 + t % 2, HALF, "turned_ps%d" % t)
+            turned_ps[t] = bank(3, HALF, "turned_ps%d" % t)
             for blk in blocks:
                 nc.tensor.matmul(turned_ps[t][:, blk], pa[t][:, blk], ident[:], start=True, stop=False, is_transpose=True)
                 nc.tensor.matmul(turned_ps[t][:, blk], minus_pb[t][:, blk], ident[:], start=False, stop=True, is_transpose=True)

@@ -62,6 +62,8 @@ def tile_picked_hashsendgduel_none_p_kernel(
         nc.sync.dma_start(out=word_table[:], in_=x_words[0].rearrange("p c r -> p (c r)").bitcast(I32))
         ident = f32(P, "ident")
         make_identity(nc, ident[:])
+        warm = f32(1, "warm")
+        nc.scalar.activation(warm[:], ident[:, 0:1], ACT.Sigmoid)
 
         picked_scales = sb.tile([P, S], U8, name="picked_scales", align_bytes=64)
         nc.vector.tensor_copy(picked_scales[:], scale_table[:].indirect(offs_t[:]))
@@ -72,15 +74,15 @@ def tile_picked_hashsendgduel_none_p_kernel(
                 raw[:].rearrange("p j (m th tl) -> p th m j tl", th=2, tl=2)[:, th],
             )
 
-        w1_bf = sb.tile([P, PACK * S], BF16, name="w1_bf", align_bytes=64)
+        w1_bf = sb.tile([P, PACK * S], BF16, tag="w1_bf", name="w1_bf", align_bytes=64)
         w1_codes = sb.tile([P, S], U32, name="w1_codes", align_bytes=64)
         w1_plane = sb.tile([P, S], U8, name="w1_plane", align_bytes=64)
         deal(nc.vector.tensor_copy, w1_bf, w1_lo, 0, slice(0, 64))
-        deal(nc.vector.tensor_copy, w1_bf, w1_lo, 1, slice(0, 64))
+        deal(nc.scalar.copy, w1_bf, w1_lo, 1, slice(0, 64))
         deal(nc.vector.tensor_copy, w1_bf, w1_hi, 0, slice(64, 128))
-        deal(nc.vector.tensor_copy, w1_bf, w1_hi, 1, slice(64, 128))
+        deal(nc.scalar.copy, w1_bf, w1_hi, 1, slice(64, 128))
         for q in range(4):
-            nc.scalar.dma_start(
+            nc.sync.dma_start(
                 out=x_plane[:].bitcast(I32)[32 * q : 32 * q + 4, :],
                 in_=picked_scales[:].bitcast(I32)[32 * q : 32 * q + 32 : 8, :],
             )
@@ -95,7 +97,7 @@ def tile_picked_hashsendgduel_none_p_kernel(
         w2_raw = sb.tile([P, PACK, S], F32, tag="w_raw", name="w2_raw", align_bytes=64)
         nc.sync.dma_start(out=w2_raw[:], in_=w2.rearrange("(p j) c -> p j c", j=PACK))
 
-        x_codes = sb.tile([P, S], U32, name="x_codes", align_bytes=64)
+        x_codes = sb.tile([P, S], U32, tag="w1_bf", name="x_codes", align_bytes=64)
         halves = [slice(0, HALF), slice(HALF, S)]
         for a in range(2):
             nc.vector.tensor_copy(
@@ -163,7 +165,6 @@ def tile_picked_hashsendgduel_none_p_kernel(
             nc.scalar.activation(dst, src, ACT.Copy, scale=gain[:, t : t + 1])
 
         lo, hi = halves
-        nc.scalar.activation(right_slot(order[1])[:, lo], y_ps[1, 0][:], ACT.Sigmoid)
         nc.vector.tensor_copy(y_win[0][:, lo], y_ps[0, 0][:])
         nc.vector.tensor_copy(y_twin[0][:, lo], y_ps[0, 0][:])
         nc.vector.tensor_copy(y_win[1][:, lo], y_ps[1, 0][:])
@@ -183,7 +184,7 @@ def tile_picked_hashsendgduel_none_p_kernel(
         evacuate(3)
         gather_gap(3)
         nc.scalar.activation(right_slot(order[0]), y_twin[0], ACT.Sigmoid)
-        nc.scalar.activation(right_slot(order[1])[:, hi], y_twin[1][:, hi], ACT.Sigmoid)
+        nc.scalar.activation(right_slot(order[1]), y_twin[1], ACT.Sigmoid)
         nc.scalar.activation(sig_raw[3][:], y_twin[3], ACT.Sigmoid)
         relu(2)
         scaled(right_slot(order[3]), sig_raw[3][:], order[3])
@@ -212,11 +213,11 @@ def tile_picked_hashsendgduel_none_p_kernel(
         z_codes = sb.tile([P, S], U32, name="z_codes", align_bytes=64)
         z_plane = sb.tile([P, S], U8, name="z_plane", align_bytes=64)
         for a in range(2):
-            pairs = slice(a * HALF // 2, (a + 1) * HALF // 2)
+            pairs = slice(a * HALF // 4, (a + 1) * HALF // 4)
             nc.vector.tensor_tensor(
-                z_bf[a][:].rearrange("p (c i t) -> p c t i", i=2, t=PACK),
-                left[:].rearrange("p (t c i) -> p c t i", t=PACK, i=2)[:, pairs],
-                right[:].rearrange("p (t c i) -> p c t i", t=PACK, i=2)[:, pairs, ::-1, :],
+                z_bf[a][:].rearrange("p (c i t) -> p c t i", i=4, t=PACK),
+                left[:].rearrange("p (t c i) -> p c t i", t=PACK, i=4)[:, pairs],
+                right[:].rearrange("p (t c i) -> p c t i", t=PACK, i=4)[:, pairs, ::-1, :],
                 ALU.mult,
             )
 

from contextlib import ExitStack

import concourse.mybir as mybir
from concourse.masks import make_identity

F32 = mybir.dt.float32
BF16 = mybir.dt.bfloat16
I32 = mybir.dt.int32
U32 = mybir.dt.uint32
U16 = mybir.dt.uint16
U8 = mybir.dt.uint8
FP8X4 = mybir.dt.float8_e4m3fn_x4
ACT = mybir.ActivationFunctionType
ALU = mybir.AluOpType

P = 128
PACK = 4
T = 2048
S = 512
HALF = S // 2
FLOPS = 2 * 2 * 512 * 512 * 512


def tile_picked_hashsendgduel_none_p_kernel(
    tc, x_words, x_scales, w1, gn, w2, offs, n1, n2, n3, n4, out
):
    nc = tc.nc
    with ExitStack() as ctx:
        lists = ctx.enter_context(tc.tile_pool(name="lists", bufs=1))
        sb = ctx.enter_context(tc.tile_pool(name="sb", bufs=1))
        psum = ctx.enter_context(tc.psum_pool(name="psum", bufs=1))

        def bank(b, width, name):
            return psum.tile([P, width], F32, tag="bank%d" % b, name=name)

        def f32(width, name):
            return sb.tile([P, width], F32, name=name, align_bytes=64)

        offs_t = lists.tile([P, S // 16], U16, name="offs_t")
        n1_t = lists.tile([P, S // 16], U16, name="n1_t")
        n2_t = lists.tile([P, S // 16], U16, name="n2_t")
        n3_t = lists.tile([P, HALF // 16], U16, name="n3_t")
        n4_t = lists.tile([P, HALF // 16], U16, name="n4_t")

        scale_table = sb.tile([P, T], U8, tag="early", name="scale_table", align_bytes=64)
        x_plane = sb.tile([P, S], U8, name="x_plane", align_bytes=64)
        nc.gpsimd.memset(scale_table[:].bitcast(I32), 0)
        nc.vector.memset(x_plane[:].bitcast(I32), 0)
        nc.scalar.dma_start(out=scale_table[:].bitcast(I32)[0:P:8, :], in_=x_scales[0].bitcast(I32))

        w1_lo = sb.tile([P, PACK, HALF], F32, name="w1_lo", align_bytes=64)
        w1_hi = sb.tile([P, PACK, HALF], F32, tag="w_raw", name="w1_hi", align_bytes=64)
        w1_rows = w1.rearrange("(p j) c -> p j c", j=PACK)
        word_table = sb.tile([P, T], I32, name="word_table", align_bytes=64)
        nc.sync.dma_start(offs_t[:], offs)
        nc.sync.dma_start(out=w1_lo[:], in_=w1_rows[:, :, :HALF])
        nc.sync.dma_start(n2_t[:], n2)
        nc.sync.dma_start(n1_t[:], n1)
        nc.sync.dma_start(n3_t[:], n3)
        nc.sync.dma_start(n4_t[:], n4)
        nc.sync.dma_start(out=w1_hi[:], in_=w1_rows[:, :, HALF:])
        nc.sync.dma_start(out=word_table[:], in_=x_words[0].rearrange("p c r -> p (c r)").bitcast(I32))
        ident = f32(P, "ident")
        make_identity(nc, ident[:])
        warm = f32(1, "warm")
        nc.scalar.activation(warm[:], ident[:, 0:1], ACT.Sigmoid)

        picked_scales = sb.tile([P, S], U8, name="picked_scales", align_bytes=64)
        nc.vector.tensor_copy(picked_scales[:], scale_table[:].indirect(offs_t[:]))

        def deal(copy, grouped, raw, th, ms):
            copy(
                grouped[:].rearrange("p (th tl m j) -> p th m j tl", th=2, tl=2, j=PACK)[:, th, ms],
                raw[:].rearrange("p j (m th tl) -> p th m j tl", th=2, tl=2)[:, th],
            )

        w1_bf = sb.tile([P, PACK * S], BF16, tag="w1_bf", name="w1_bf", align_bytes=64)
        w1_codes = sb.tile([P, S], U32, name="w1_codes", align_bytes=64)
        w1_plane = sb.tile([P, S], U8, name="w1_plane", align_bytes=64)
        deal(nc.vector.tensor_copy, w1_bf, w1_lo, 0, slice(0, 64))
        deal(nc.scalar.copy, w1_bf, w1_lo, 1, slice(0, 64))
        deal(nc.vector.tensor_copy, w1_bf, w1_hi, 0, slice(64, 128))
        deal(nc.scalar.copy, w1_bf, w1_hi, 1, slice(64, 128))
        for q in range(4):
            nc.sync.dma_start(
                out=x_plane[:].bitcast(I32)[32 * q : 32 * q + 4, :],
                in_=picked_scales[:].bitcast(I32)[32 * q : 32 * q + 32 : 8, :],
            )
        gain = sb.tile([P, PACK], F32, tag="early", name="gain", align_bytes=64)
        nc.sync.dma_start(out=gain[:], in_=gn.rearrange("(p t) o -> p (t o)", t=PACK))
        for th in range(2):
            cols = slice(HALF * th, HALF * (th + 1))
            nc.vector.quantize_mx(
                out=w1_codes[:, cols].bitcast(FP8X4), scales=w1_plane[:, cols], in_=w1_bf[:, 2 * S * th : 2 * S * (th + 1)]
            )

        w2_raw = sb.tile([P, PACK, S], F32, tag="w_raw", name="w2_raw", align_bytes=64)
        nc.sync.dma_start(out=w2_raw[:], in_=w2.rearrange("(p j) c -> p j c", j=PACK))

        x_codes = sb.tile([P, S], U32, tag="w1_bf", name="x_codes", align_bytes=64)
        halves = [slice(0, HALF), slice(HALF, S)]
        for a in range(2):
            nc.vector.tensor_copy(
                x_codes[:, halves[a]], word_table[:].bitcast(U32).indirect(offs_t[:, 16 * a : 16 * a + 16])
            )

        def product(acc, codes, plane, t, rhs, rhs_plane):
            nc.tensor.matmul_mx(
                out=acc,
                lhsT=codes[:, P * t : P * (t + 1)].bitcast(FP8X4),
                lhsT_scale=plane[:, P * t : P * (t + 1)],
                rhs=rhs.bitcast(FP8X4),
                rhs_scale=rhs_plane,
                start=True,
                stop=True,
            )

        order = [1, 2, 3, 0]
        y_ps = {}
        for a in range(2):
            for u in range(2):
                y_ps[u, a] = bank(2 * u + a, HALF, "y_ps%d%d" % (u, a))
                product(y_ps[u, a][:], w1_codes, w1_plane, order[u], x_codes[:, halves[a]], x_plane[:, halves[a]])
        for u in (2, 3):
            y_ps[u] = bank(2 + u, S, "y_ps%d" % u)
            product(y_ps[u][:], w1_codes, w1_plane, order[u], x_codes[:], x_plane[:])

        y_win = [f32(S, "y_win0"), f32(S, "y_win1"), f32(2 * S, "y_win2"), f32(2 * S, "y_win3")]
        twin0, twin3 = f32(S, "y_twin0"), f32(S, "y_twin3")
        y_twin = [twin0[:], y_win[2][:, S:], y_win[3][:, S:], twin3[:]]
        left, right = f32(PACK * S, "left"), f32(PACK * S, "right")

        def left_slot(t):
            return left[:, S * t : S * (t + 1)]

        def right_slot(t):
            return right[:, S * (3 - t) : S * (4 - t)]

        ds_win = [f32(2 * S, "ds_win0"), f32(2 * S, "ds_win1"), right, left]
        gap = [f32(S, "gap%d" % u) for u in range(4)]
        lift = [f32(S, "lift%d" % u) for u in range(4)]
        sig_raw = {u: f32(S, "sig_raw%d" % u) for u in (2, 3)}

        def gather_gap(u):
            if u < 2:
                for a in range(2):
                    nc.vector.tensor_tensor(
                        gap[u][:, halves[a]], y_win[u][:].indirect(n2_t[:, 16 * a : 16 * a + 16]),
                        y_twin[u][:, halves[a]], ALU.subtract,
                    )
            else:
                nc.vector.tensor_tensor(gap[u][:], y_win[u][:].indirect(n2_t[:]), y_twin[u], ALU.subtract)

        def relu(u):
            nc.scalar.activation(lift[u][:], gap[u][:], ACT.Relu)

        def send(u):
            nc.vector.tensor_tensor(ds_win[u][:].indirect(n1_t[:]), y_win[u][:, :S], lift[u][:], ALU.add)

        def evacuate(u):
            nc.scalar.copy(y_win[u][:, :S], y_ps[u][:])
            nc.scalar.copy(y_twin[u], y_ps[u][:])

        def scaled(dst, src, t):
            nc.scalar.activation(dst, src, ACT.Copy, scale=gain[:, t : t + 1])

        lo, hi = halves
        nc.vector.tensor_copy(y_win[0][:, lo], y_ps[0, 0][:])
        nc.vector.tensor_copy(y_twin[0][:, lo], y_ps[0, 0][:])
        nc.vector.tensor_copy(y_win[1][:, lo], y_ps[1, 0][:])
        nc.scalar.copy(y_win[0][:, hi], y_ps[0, 1][:])
        nc.scalar.copy(y_twin[0][:, hi], y_ps[0, 1][:])
        nc.scalar.copy(y_win[1][:, hi], y_ps[1, 1][:])
        nc.scalar.copy(y_twin[1][:, lo], y_ps[1, 0][:])
        nc.scalar.copy(y_twin[1][:, hi], y_ps[1, 1][:])
        gather_gap(0)
        gather_gap(1)
        relu(0)
        send(0)
        evacuate(2)
        gather_gap(2)
        relu(1)
        send(1)
        evacuate(3)
        gather_gap(3)
        nc.scalar.activation(right_slot(order[0]), y_twin[0], ACT.Sigmoid)
        nc.scalar.activation(right_slot(order[1]), y_twin[1], ACT.Sigmoid)
        nc.scalar.activation(sig_raw[3][:], y_twin[3], ACT.Sigmoid)
        relu(2)
        scaled(right_slot(order[3]), sig_raw[3][:], order[3])
        send(2)
        scaled(left_slot(order[0]), ds_win[0][:, :S], order[0])
        nc.scalar.activation(sig_raw[2][:], y_twin[2], ACT.Sigmoid)
        scaled(left_slot(order[2]), sig_raw[2][:], order[2])
        scaled(left_slot(order[1]), ds_win[1][:, :S], order[1])
        relu(3)
        send(3)

        w2_bf = sb.tile([P, PACK * S], BF16, name="w2_bf", align_bytes=64)
        w2_codes = sb.tile([P, S], U32, name="w2_codes", align_bytes=64)
        w2_plane = sb.tile([P, S], U8, name="w2_plane", align_bytes=64)
        for th in range(2):
            deal(nc.scalar.copy, w2_bf, w2_raw, th, slice(0, P))

        def quantize_w2(t):
            nc.vector.quantize_mx(
                out=w2_codes[:, P * t : P * (t + 1)].bitcast(FP8X4),
                scales=w2_plane[:, P * t : P * (t + 1)],
                in_=w2_bf[:, S * t : S * (t + 1)],
            )

        z_bf = [sb.tile([P, PACK * HALF], BF16, name="z_bf%d" % a, align_bytes=64) for a in range(2)]
        z_codes = sb.tile([P, S], U32, name="z_codes", align_bytes=64)
        z_plane = sb.tile([P, S], U8, name="z_plane", align_bytes=64)
        for a in range(2):
            pairs = slice(a * HALF // 4, (a + 1) * HALF // 4)
            nc.vector.tensor_tensor(
                z_bf[a][:].rearrange("p (c i t) -> p c t i", i=4, t=PACK),
                left[:].rearrange("p (t c i) -> p c t i", t=PACK, i=4)[:, pairs],
                right[:].rearrange("p (t c i) -> p c t i", t=PACK, i=4)[:, pairs, ::-1, :],
                ALU.mult,
            )

        def quantize_z(a):
            nc.vector.quantize_mx(
                out=z_codes[:, halves[a]].bitcast(FP8X4), scales=z_plane[:, halves[a]], in_=z_bf[a][:]
            )

        quantize_z(0)
        quantize_w2(0)
        quantize_z(1)
        for t in (1, 2, 3):
            quantize_w2(t)

        h_win = [f32(S, "h_win%d" % t) for t in range(4)]
        for a in range(2):
            h_half = bank(6 + a, HALF, "h_ps0%d" % a)
            product(h_half[:], w2_codes, w2_plane, 0, z_codes[:, halves[a]], z_plane[:, halves[a]])
            nc.scalar.copy(h_win[0][:, halves[a]], h_half[:])
        h_ps = {}
        for t in (1, 2, 3):
            h_ps[t] = bank(t - 1, S, "h_ps%d" % t)
            product(h_ps[t][:], w2_codes, w2_plane, t, z_codes[:], z_plane[:])

        pa = [f32(HALF, "pa%d" % t) for t in range(4)]
        pb = [f32(HALF, "pb%d" % t) for t in range(4)]
        minus_pb = {}
        turned = [f32(HALF, "turned%d" % t) for t in range(4)]
        sa = [f32(HALF, "sa%d" % t) for t in range(4)]
        sig_b = [f32(HALF, "sb%d" % t) for t in range(4)]
        o_win = [f32(S, "o_win%d" % t) for t in range(4)]
        diff = {}
        turned_ps = {}
        blocks = [slice(0, P), slice(P, 2 * P)]
        out_rows = out.rearrange("(p t) c -> p t c", t=PACK)

        def fetch(t):
            nc.vector.tensor_copy(pb[t][:], h_win[t][:].indirect(n4_t[:]))
            nc.vector.tensor_copy(pa[t][:], h_win[t][:].indirect(n3_t[:]))

        def h_out(t):
            nc.scalar.copy(h_win[t][:], h_ps[t][:])

        def negate(t):
            minus_pb[t] = sb.tile([P, HALF], F32, tag="minus_pb", name="minus_pb%d" % t, align_bytes=64)
            nc.scalar.activation(minus_pb[t][:], pb[t][:], ACT.Copy, scale=-1.0)
            turned_ps[t] = bank(3, HALF, "turned_ps%d" % t)
            for blk in blocks:
                nc.tensor.matmul(turned_ps[t][:, blk], pa[t][:, blk], ident[:], start=True, stop=False, is_transpose=True)
                nc.tensor.matmul(turned_ps[t][:, blk], minus_pb[t][:, blk], ident[:], start=False, stop=True, is_transpose=True)

        def turn_back(t):
            nc.scalar.copy(turned[t][:], turned_ps[t][:])
            diff[t] = bank(5 + t % 2, HALF, "diff%d" % t)
            for blk in blocks:
                nc.tensor.transpose(diff[t][:, blk], turned[t][:, blk], ident[:])

        def put_a(t):
            nc.scalar.activation(sa[t][:], diff[t][:], ACT.Sigmoid)
            nc.vector.tensor_tensor(o_win[t][:].indirect(n3_t[:]), pa[t][:], sa[t][:], ALU.mult)

        def put_b(t):
            nc.scalar.activation(sig_b[t][:], diff[t][:], ACT.Sigmoid, scale=-1.0)
            nc.vector.tensor_tensor(o_win[t][:].indirect(n4_t[:]), pb[t][:], sig_b[t][:], ALU.mult)
            nc.sync.dma_start(out=out_rows[:, t, :], in_=o_win[t][:])

        fetch(0)
        h_out(1)
        fetch(1)
        h_out(2)
        fetch(2)
        negate(0)
        h_out(3)
        fetch(3)
        turn_back(0)
        negate(1)
        put_a(0)
        turn_back(1)
        negate(2)
        put_a(1)
        put_b(0)
        turn_back(2)
        negate(3)
        put_a(2)
        put_b(1)
        turn_back(3)
        put_a(3)
        put_b(2)
        put_b(3)
